import numpy as np
import ml_dtypes


def mxq(x, axis, fmt="e4m3"):
    dtype, down = {"e4m3": (ml_dtypes.float8_e4m3fn, 7), "e5m2": (ml_dtypes.float8_e5m2, 14)}[fmt]
    v = np.moveaxis(np.asarray(x, np.float32).astype(ml_dtypes.bfloat16).astype(np.float64), axis, -1)
    blocks = v.reshape(v.shape[:-1] + (-1, 32))
    amax = np.abs(blocks).max(-1, keepdims=True)
    byte = np.maximum(np.where(amax > 0, np.frexp(amax)[1] - 1 + 127, 0) - down, 1)
    scale = np.exp2(byte - 127.0)
    codes = (blocks / scale).astype(np.float32).astype(dtype).astype(np.float64)
    return np.moveaxis((codes * scale).reshape(v.shape), -1, axis)


WIDE = False


def mx_kscale(k):
    if not WIDE:
        return np.ones(k)
    levels = np.array([10, -10, 5, -5, 0])
    if k % 512:
        return np.exp2(np.random.permutation(np.resize(levels, k // 32))).repeat(32)
    a = np.empty((k // 512, 16))
    for p in range(k // 512):
        a[p, :8] = np.random.permutation(np.resize(levels, 8))
        for g in range(8):
            far = levels[np.abs(levels - a[p, g]) >= 10]
            a[p, g + 8] = far[np.random.randint(len(far))]
    return np.exp2(a.ravel()).repeat(32)


def f64(x):
    return np.asarray(x).astype(np.float64)


def striped(idx):
    return np.tile(idx.reshape(-1, 16).T, (8, 1)).astype(np.uint16)


def unstriped(offs):
    return offs[:16].T.reshape(-1).astype(np.int64)


E2M1 = np.array([0.0, 0.5, 1.0, 1.5, 2.0, 3.0, 4.0, 6.0, -0.0, -0.5, -1.0, -1.5, -2.0, -3.0, -4.0, -6.0])


def pack_weight(w, fmt):
    k, n = w.shape
    w = f64(np.asarray(w, np.float32).astype(ml_dtypes.bfloat16)).reshape(k // 32, 32, n)
    amax = np.abs(w).max(1)
    if fmt == "e4m3":
        byte = np.frexp(amax)[1] - 1 + 127 - 7
    else:
        mant, ex = np.frexp(amax / 6.0)
        byte = np.where(mant > 0.5, ex, ex - 1) + 127
    byte = np.clip(np.where(amax > 0, byte, 1), 1, 254)
    scaled = (w * np.exp2(127.0 - byte)[:, None, :]).reshape(k, n).astype(np.float32)
    by_word = np.ascontiguousarray(scaled.reshape(k // 512, 128, 4, n).transpose(0, 1, 3, 2))
    if fmt == "e4m3":
        words = by_word.astype(ml_dtypes.float8_e4m3fn).view(np.uint8)
    else:
        c = by_word.astype(ml_dtypes.float4_e2m1fn).view(np.uint8) & 0xF
        words = (c[..., 0::2] | (c[..., 1::2] << 4)).reshape(k // 512, 128, 2 * n)
    return np.ascontiguousarray(words), np.ascontiguousarray(byte.astype(np.uint8).reshape(k // 512, 16, n))


def unpack_weight(words, scales, fmt):
    g, _, n = scales.shape
    words = np.ascontiguousarray(words).reshape(g, 128, n, -1)
    if fmt == "e4m3":
        vals = words.view(ml_dtypes.float8_e4m3fn).astype(np.float64)
    else:
        nib = np.empty((g, 128, n, 4), np.uint8)
        nib[..., 0::2] = words & 0xF
        nib[..., 1::2] = words >> 4
        vals = E2M1[nib]
    vals = vals * np.repeat(np.exp2(scales.astype(np.float64) - 127.0), 8, axis=1)[..., None]
    return vals.transpose(0, 1, 3, 2).reshape(g * 512, n)


def relu(v):
    return np.maximum(v, 0.0)


K, T, E1, C1, E2, C2, H = 1024, 512, 2, 256, 4, 128, 512
N = 512


def by_expert(wq, xq, E, C):
    return np.concatenate([wq[e].T @ xq[:, e * C:(e + 1) * C] for e in range(E)], axis=1)


def setup_inputs():
    n = np.random.standard_normal
    s = mx_kscale(K)
    u = mx_kscale(H)
    slots1, slots2 = np.random.permutation(T), np.random.permutation(T)
    x = pack_weight(n((K, T)) * s[:, None], "e4m3")
    wa = [pack_weight(m, "e4m3") for m in n((E1, K, H)) / np.sqrt(K) / s[None, :, None]]
    wb = [pack_weight(m, "e2m1") for m in n((E2, K, H)) / np.sqrt(K) / s[None, :, None] * u]
    w2 = pack_weight(n((H, N)) / np.sqrt(H) / u[:, None], "e4m3")
    return {
        "x_words": x[0],
        "x_scales": x[1],
        "wa_words": np.stack([m[0] for m in wa]),
        "wa_scales": np.stack([m[1] for m in wa]),
        "wb_words": np.stack([m[0] for m in wb]),
        "wb_scales": np.stack([m[1] for m in wb]),
        "w2_words": w2[0],
        "w2_scales": w2[1],
        "offs": striped(slots1),
        "offs2": striped(slots2),
    }


def reference(x_words, x_scales, wa_words, wa_scales, wb_words, wb_scales, w2_words, w2_scales, offs, offs2):
    wa = np.stack([unpack_weight(wa_words[e], wa_scales[e], "e4m3") for e in range(E1)])
    wb = np.stack([unpack_weight(wb_words[e], wb_scales[e], "e2m1") for e in range(E2)])
    w2 = unpack_weight(w2_words, w2_scales, "e4m3")
    idx, idx2 = unstriped(offs), unstriped(offs2)
    x = unpack_weight(x_words, x_scales, "e4m3")
    a, c = np.zeros((H, T)), np.zeros((H, T))
    a[:, idx] = by_expert(wa, x[:, idx], E1, C1)
    c[:, idx2] = by_expert(wb, x[:, idx2], E2, C2)
    return w2.T @ mxq(relu(a) * c, 0, "e4m3")

@@ -1,0 +1,217 @@
+from contextlib import ExitStack
+
+import concourse.mybir as mybir
+from concourse.masks import make_identity
+
+K, T, H, N = 1024, 512, 512, 512
+E1, C1, E2, C2 = 2, 256, 4, 128
+FLOPS = 2 * T * (2 * K * H + H * N)
+
+F32 = mybir.dt.float32
+BF16 = mybir.dt.bfloat16
+I32 = mybir.dt.int32
+U32 = mybir.dt.uint32
+U16 = mybir.dt.uint16
+U8 = mybir.dt.uint8
+FP8X4 = mybir.dt.float8_e4m3fn_x4
+FP4X4 = mybir.dt.float4_e2m1fn_x4
+RELU = mybir.ActivationFunctionType.Relu
+MULT = mybir.AluOpType.mult
+
+P = 128
+PASSES = 2
+WIDE = 704
+CHUNKS = (256, 128, 128)
+
+
+def tile_moe_pool_relu_kernel(
+    tc, x_words, x_scales, wa_words, wa_scales, wb_words, wb_scales, w2_words, w2_scales, offs, offs2, out
+):
+    nc = tc.nc
+    with ExitStack() as ctx:
+        lists = ctx.enter_context(tc.tile_pool(name="lists", bufs=1))
+        sb = ctx.enter_context(tc.tile_pool(name="sb", bufs=1))
+        ps = ctx.enter_context(tc.psum_pool(name="ps", bufs=1))
+
+        def tile(shape, dtype, name):
+            return sb.tile(shape, dtype, name=name, align_bytes=64)
+
+        list_a = lists.tile([P, T // 16], U16, name="list_a")
+        list_b = lists.tile([P, T // 16], U16, name="list_b")
+        banks = [ps.tile([P, 512], F32, name="bank%d" % b) for b in range(8)]
+
+        xw = [tile([P, WIDE], I32, "xw%d" % s) for s in range(PASSES)]
+        xs = tile([P, WIDE], U8, "xs")
+        wa = [tile([P, PASSES, H], I32, "wa%d" % e) for e in range(E1)]
+        was = tile([P, H], U8, "was")
+        wb = tile([P, E2 * PASSES, 2 * H], U8, "wb")
+        wbs = tile([P, E2 * PASSES, H], U8, "wbs")
+        w2 = tile([P, N], I32, "w2")
+        w2s = tile([P, N], U8, "w2s")
+        xb_s1 = tile([P, T], U8, "xb_s1")
+        ident = tile([P, P], F32, "ident")
+
+        nc.vector.memset(xs[:].bitcast(I32), 0)
+        nc.vector.memset(was[:].bitcast(I32), 0)
+        for s in range(PASSES):
+            nc.vector.memset(xw[s][:, T:WIDE], 0)
+        nc.vector.memset(wbs[:].rearrange("p g i -> p (g i)").bitcast(I32), 0)
+        nc.vector.memset(w2s[:].bitcast(I32), 0)
+        nc.vector.memset(xb_s1[:].bitcast(I32), 0)
+        make_identity(nc, ident[:])
+
+        def load_x(s):
+            nc.sync.dma_start(xw[s][:, 0:T], x_words[s].rearrange("p t d -> p (t d)").bitcast(I32))
+
+        def load_wa(e):
+            nc.sync.dma_start(wa[e][:], wa_words[e].rearrange("s p i d -> p s (i d)").bitcast(I32))
+
+        nc.sync.dma_start(list_a[:], offs)
+        load_x(0)
+        for q in range(4):
+            nc.sync.dma_start(
+                xs[32 * q : 32 * q + 8, 0:T].bitcast(I32), x_scales[:, 4 * q : 4 * q + 4, :].bitcast(I32)
+            )
+        load_x(1)
+        load_wa(0)
+        was_rows = wa_scales.rearrange("e s b i -> (e s) b i")
+        for q in range(4):
+            nc.sync.dma_start(
+                was[32 * q : 32 * q + 16, :].bitcast(I32), was_rows[:, 4 * q : 4 * q + 4, :].bitcast(I32)
+            )
+        nc.sync.dma_start(list_b[:], offs2)
+        load_wa(1)
+        nc.sync.dma_start(wb[:].bitcast(I32), wb_words.rearrange("f s p b -> p (f s) b").bitcast(I32))
+        wbs_rows = wb_scales.rearrange("f s b i -> b (f s) i")
+        for q in range(4):
+            nc.sync.dma_start(
+                wbs[32 * q : 32 * q + 4, :, :].bitcast(I32), wbs_rows[4 * q : 4 * q + 4, :, :].bitcast(I32)
+            )
+        nc.sync.dma_start(w2[:], w2_words[0].rearrange("p n d -> p (n d)").bitcast(I32))
+        for q in range(4):
+            nc.sync.dma_start(
+                w2s[32 * q : 32 * q + 4, :].bitcast(I32), w2_scales[0, 4 * q : 4 * q + 4, :].bitcast(I32)
+            )
+
+        xa = [[tile([P, C1], U32, "xa%d%d" % (e, s)) for s in range(PASSES)] for e in range(E1)]
+        xa_s = [tile([P, C1], U8, "xa_s%d" % e) for e in range(E1)]
+        for e in range(E1):
+            part = list_a[:, 16 * e : 16 * (e + 1)]
+            for s in range(PASSES):
+                nc.vector.tensor_copy(xa[e][s][:], xw[s][:, 0:T].bitcast(U32).indirect(part))
+            nc.vector.tensor_copy(xa_s[e][:], xs[:, 0:T].indirect(part))
+        xb = [tile([P, T], U32, "xb%d" % s) for s in range(PASSES)]
+        xb_s = tile([P, T], U8, "xb_s")
+        nc.vector.tensor_copy(xb_s[:], xs[:].indirect(list_b[:]))
+        nc.sync.dma_start(xb_s1[0 : P - 4, :].bitcast(I32), xb_s[4:P, :].bitcast(I32))
+        for s in range(PASSES):
+            nc.vector.tensor_copy(xb[s][:], xw[s][:].bitcast(U32).indirect(list_b[:]))
+
+        turned = [tile([P, 4, P], F32, "turned%d" % b) for b in range(8)]
+
+        def by_plane(bank):
+            return bank[:].rearrange("p (q r) -> p r q", r=4)
+
+        for b in range(4):
+            e, cols = b // 2, slice(P * (b % 2), P * (b % 2 + 1))
+            acc = banks[b % 3]
+            for s in range(PASSES):
+                nc.tensor.matmul_mx(
+                    out=acc[:],
+                    lhsT=xa[e][s][:, cols].bitcast(FP8X4),
+                    lhsT_scale=xa_s[e][4 * s : P, cols],
+                    rhs=wa[e][:, s, :].bitcast(FP8X4),
+                    rhs_scale=was[4 * (2 * e + s) : P, :],
+                    start=(s == 0),
+                    stop=(s == PASSES - 1),
+                )
+            nc.scalar.activation(turned[b][:], by_plane(acc), RELU)
+            for r in (1, 2):
+                c0 = C1 * (r - 1) + P * (b % 2)
+                nc.tensor.transpose(banks[3 + e][:, c0 : c0 + P], turned[b][:, r, :], ident[:])
+            nc.tensor.transpose(banks[5][:, P * b : P * (b + 1)], turned[b][:, 3, :], ident[:])
+            nc.tensor.transpose(banks[6][:, P * b : P * (b + 1)], turned[b][:, 0, :], ident[:])
+
+        src = [tile([P, T], F32, "src%d" % i) for i in range(2)]
+        a_all = tile([P, 4 * T], F32, "a_all")
+        c_all = tile([P, 4 * T], F32, "c_all")
+        a_win = {r: tile([P, WIDE], F32, "a_win%d" % r) for r in (1, 2, 3)}
+        c_win = [tile([P, WIDE], F32, "c_win%d" % r) for r in range(4)]
+
+        for e in range(E1):
+            nc.scalar.copy(src[e][:], banks[3 + e][:])
+            for r in (1, 2):
+                nc.vector.tensor_copy(
+                    a_win[r][:].indirect(list_a[:, 16 * e : 16 * (e + 1)]), src[e][:, C1 * (r - 1) : C1 * r]
+                )
+        nc.scalar.copy(src[0][:], banks[5][:])
+        nc.vector.tensor_copy(a_win[3][:].indirect(list_a[:]), src[0][:])
+        for r in (1, 2, 3):
+            nc.sync.dma_start(a_all[:, T * r : T * (r + 1)], a_win[r][:, 0:T])
+
+        b_bank = [banks[7], banks[3], banks[4], banks[5]]
+        for f in range(E2):
+            cols = slice(P * f, P * (f + 1))
+            acc = banks[(4 + f) % 3]
+            for s in range(PASSES):
+                nc.tensor.matmul_mx(
+                    out=acc[:],
+                    lhsT=xb[s][:, cols].bitcast(FP8X4),
+                    lhsT_scale=(xb_s, xb_s1)[s][:, cols],
+                    rhs=wb[:, 2 * f + s, :].bitcast(FP4X4),
+                    rhs_scale=wbs[:, 2 * f + s, :],
+                    start=(s == 0),
+                    stop=(s == PASSES - 1),
+                )
+            nc.scalar.copy(turned[4 + f][:], by_plane(acc))
+            for r in range(4):
+                nc.tensor.transpose(b_bank[r][:, cols], turned[4 + f][:, r, :], ident[:])
+        for r in range(4):
+            stage = src[(r + 1) % 2]
+            nc.scalar.copy(stage[:], b_bank[r][:])
+            nc.vector.tensor_copy(c_win[r][:].indirect(list_b[:]), stage[:])
+            nc.scalar.copy(c_all[:, T * r : T * (r + 1)], c_win[r][:, 0:T])
+        nc.scalar.copy(src[1][:], banks[6][:])
+        nc.vector.tensor_copy(a_all[:].indirect(list_a[:]), src[1][:])
+
+        a4 = a_all[:].rearrange("p (r c i) -> p c r i", r=4, i=4)
+        c4 = c_all[:].rearrange("p (r c i) -> p c r i", r=4, i=4)
+        out_v = out.rearrange("(n p) t -> p n t", p=P)
+        hs = []
+        t0 = 0
+        for j, w in enumerate(CHUNKS):
+            h = tile([P, 4 * w], BF16, "h%d" % j)
+            cs = slice(t0 // 4, (t0 + w) // 4)
+            nc.vector.tensor_tensor(
+                h[:].rearrange("p (c i r) -> p c r i", i=4, r=4), a4[:, cs, :, :], c4[:, cs, :, :], MULT
+            )
+            hs.append((h, t0, w))
+            t0 = t0 + w
+        bank_at = 0
+        for j, (h, t0, w) in enumerate(hs):
+            hq = tile([P, w], U32, "hq%d" % j)
+            hq_s = tile([P, w], U8, "hq_s%d" % j)
+            nc.vector.quantize_mx(out=hq[:].bitcast(FP8X4), scales=hq_s[:], in_=h[:])
+            res = tile([P, 4, w], F32, "res%d" % j)
+            last = j == len(hs) - 1
+            per_bank = 2 if (w == 256 or last) else 4
+            for n0 in range(0, 4, per_bank):
+                acc = banks[bank_at]
+                bank_at = bank_at + 1
+                for n in range(n0, n0 + per_bank):
+                    nc.tensor.matmul_mx(
+                        out=acc[:, w * (n - n0) : w * (n - n0 + 1)],
+                        lhsT=w2[:, P * n : P * (n + 1)].bitcast(FP8X4),
+                        lhsT_scale=w2s[:, P * n : P * (n + 1)],
+                        rhs=hq[:].bitcast(FP8X4),
+                        rhs_scale=hq_s[:],
+                        start=True,
+                        stop=True,
+                    )
+                got = acc[:, 0 : w * per_bank].rearrange("p (n t) -> p n t", t=w)
+                dst = res[:, n0 : n0 + per_bank, :]
+                if last and n0 > 0:
+                    nc.vector.tensor_copy(dst, got)
+                else:
+                    nc.scalar.copy(dst, got)
+                nc.sync.dma_start(out_v[:, n0 : n0 + per_bank, t0 : t0 + w], dst)

@@ -21,7 +21,9 @@ MULT = mybir.AluOpType.mult
 P = 128
 PASSES = 2
 WIDE = 704
-CHUNKS = (256, 128, 128)
+WARM = 5
+RUN = 2
+CHUNKS = (128, 128, 256)
 
 
 def tile_moe_pool_relu_kernel(
@@ -40,28 +42,27 @@ def tile_moe_pool_relu_kernel(
         list_b = lists.tile([P, T // 16], U16, name="list_b")
         banks = [ps.tile([P, 512], F32, name="bank%d" % b) for b in range(8)]
 
-        xw = [tile([P, WIDE], I32, "xw%d" % s) for s in range(PASSES)]
+        xw = tile([P, T + WIDE], I32, "xw")
+        xw_at = (T, 0)
         xs = tile([P, WIDE], U8, "xs")
         wa = [tile([P, PASSES, H], I32, "wa%d" % e) for e in range(E1)]
-        was = tile([P, H], U8, "was")
+        wsc = tile([P, (2 + E2 * PASSES) * H], U8, "wsc")
+        was = wsc[:, 0:H]
+        w2s = wsc[:, H : 2 * H]
+        wbs = wsc[:, 2 * H :].rearrange("p (g i) -> p g i", i=H)
         wb = tile([P, E2 * PASSES, 2 * H], U8, "wb")
-        wbs = tile([P, E2 * PASSES, H], U8, "wbs")
         w2 = tile([P, N], I32, "w2")
-        w2s = tile([P, N], U8, "w2s")
         xb_s1 = tile([P, T], U8, "xb_s1")
         ident = tile([P, P], F32, "ident")
 
         nc.vector.memset(xs[:].bitcast(I32), 0)
-        nc.vector.memset(was[:].bitcast(I32), 0)
-        for s in range(PASSES):
-            nc.vector.memset(xw[s][:, T:WIDE], 0)
-        nc.vector.memset(wbs[:].rearrange("p g i -> p (g i)").bitcast(I32), 0)
-        nc.vector.memset(w2s[:].bitcast(I32), 0)
+        nc.vector.memset(xw[:, 2 * T : T + WIDE], 0)
+        nc.vector.memset(wsc[:].bitcast(I32), 0)
         nc.vector.memset(xb_s1[:].bitcast(I32), 0)
         make_identity(nc, ident[:])
 
         def load_x(s):
-            nc.sync.dma_start(xw[s][:, 0:T], x_words[s].rearrange("p t d -> p (t d)").bitcast(I32))
+            nc.sync.dma_start(xw[:, xw_at[s] : xw_at[s] + T], x_words[s].rearrange("p t d -> p (t d)").bitcast(I32))
 
         def load_wa(e):
             nc.sync.dma_start(wa[e][:], wa_words[e].rearrange("s p i d -> p s (i d)").bitcast(I32))
@@ -93,44 +94,26 @@ def tile_moe_pool_relu_kernel(
                 w2s[32 * q : 32 * q + 4, :].bitcast(I32), w2_scales[0, 4 * q : 4 * q + 4, :].bitcast(I32)
             )
 
-        xa = [[tile([P, C1], U32, "xa%d%d" % (e, s)) for s in range(PASSES)] for e in range(E1)]
-        xa_s = [tile([P, C1], U8, "xa_s%d" % e) for e in range(E1)]
+        def x_window(s):
+            return xw[:, xw_at[s] : xw_at[s] + WIDE].bitcast(U32)
+
+        xa = [tile([P, T], U32, "xa%d" % s) for s in range(PASSES)]
+        xa_s = tile([P, T], U8, "xa_s")
+        nc.vector.tensor_copy(xa[0][:], x_window(0).indirect(list_a[:]))
+        nc.vector.tensor_copy(xa_s[:], xs[:].indirect(list_a[:]))
         for e in range(E1):
-            part = list_a[:, 16 * e : 16 * (e + 1)]
-            for s in range(PASSES):
-                nc.vector.tensor_copy(xa[e][s][:], xw[s][:, 0:T].bitcast(U32).indirect(part))
-            nc.vector.tensor_copy(xa_s[e][:], xs[:, 0:T].indirect(part))
+            nc.vector.tensor_copy(xa[1][:, C1 * e : C1 * (e + 1)], x_window(1).indirect(list_a[:, 16 * e : 16 * (e + 1)]))
         xb = [tile([P, T], U32, "xb%d" % s) for s in range(PASSES)]
         xb_s = tile([P, T], U8, "xb_s")
         nc.vector.tensor_copy(xb_s[:], xs[:].indirect(list_b[:]))
         nc.sync.dma_start(xb_s1[0 : P - 4, :].bitcast(I32), xb_s[4:P, :].bitcast(I32))
         for s in range(PASSES):
-            nc.vector.tensor_copy(xb[s][:], xw[s][:].bitcast(U32).indirect(list_b[:]))
+            nc.vector.tensor_copy(xb[s][:], x_window(s).indirect(list_b[:]))
 
         turned = [tile([P, 4, P], F32, "turned%d" % b) for b in range(8)]
 
         def by_plane(bank):
             return bank[:].rearrange("p (q r) -> p r q", r=4)
-
-        for b in range(4):
-            e, cols = b // 2, slice(P * (b % 2), P * (b % 2 + 1))
-            acc = banks[b % 3]
-            for s in range(PASSES):
-                nc.tensor.matmul_mx(
-                    out=acc[:],
-                    lhsT=xa[e][s][:, cols].bitcast(FP8X4),
-                    lhsT_scale=xa_s[e][4 * s : P, cols],
-                    rhs=wa[e][:, s, :].bitcast(FP8X4),
-                    rhs_scale=was[4 * (2 * e + s) : P, :],
-                    start=(s == 0),
-                    stop=(s == PASSES - 1),
-                )
-            nc.scalar.activation(turned[b][:], by_plane(acc), RELU)
-            for r in (1, 2):
-                c0 = C1 * (r - 1) + P * (b % 2)
-                nc.tensor.transpose(banks[3 + e][:, c0 : c0 + P], turned[b][:, r, :], ident[:])
-            nc.tensor.transpose(banks[5][:, P * b : P * (b + 1)], turned[b][:, 3, :], ident[:])
-            nc.tensor.transpose(banks[6][:, P * b : P * (b + 1)], turned[b][:, 0, :], ident[:])
 
         src = [tile([P, T], F32, "src%d" % i) for i in range(2)]
         a_all = tile([P, 4 * T], F32, "a_all")
@@ -138,12 +121,42 @@ def tile_moe_pool_relu_kernel(
         a_win = {r: tile([P, WIDE], F32, "a_win%d" % r) for r in (1, 2, 3)}
         c_win = [tile([P, WIDE], F32, "c_win%d" % r) for r in range(4)]
 
-        for e in range(E1):
-            nc.scalar.copy(src[e][:], banks[3 + e][:])
-            for r in (1, 2):
-                nc.vector.tensor_copy(
-                    a_win[r][:].indirect(list_a[:, 16 * e : 16 * (e + 1)]), src[e][:, C1 * (r - 1) : C1 * r]
+        def expert_a(b):
+            e, cols = b // 2, slice(P * b, P * (b + 1))
+            acc = banks[b % 2]
+            for s in range(PASSES):
+                nc.tensor.matmul_mx(
+                    out=acc[:],
+                    lhsT=xa[s][:, cols].bitcast(FP8X4),
+                    lhsT_scale=xa_s[4 * s : P, cols],
+                    rhs=wa[e][:, s, :].bitcast(FP8X4),
+                    rhs_scale=was[4 * (2 * e + s) : P, :],
+                    start=(s == 0),
+                    stop=(s == PASSES - 1),
                 )
+            nc.scalar.activation(turned[b][:], by_plane(acc), RELU)
+
+        def early_planes(blocks, bank, stage):
+            w = P * len(blocks)
+            for j, b in enumerate(blocks):
+                for r in (1, 2):
+                    c0 = w * (r - 1) + P * j
+                    nc.tensor.transpose(bank[:, c0 : c0 + P], turned[b][:, r, :], ident[:])
+            nc.scalar.copy(stage, bank[:, 0 : 2 * w])
+            part = list_a[:, 8 * blocks[0] : 8 * (blocks[-1] + 1)]
+            for r in (1, 2):
+                nc.vector.tensor_copy(a_win[r][:].indirect(part), stage[:, w * (r - 1) : w * r])
+
+        expert_a(0)
+        expert_a(1)
+        early_planes([0], banks[7], src[0][:, 0 : 2 * P])
+        early_planes([1], banks[3], src[0][:, 2 * P : 4 * P])
+        expert_a(2)
+        expert_a(3)
+        early_planes([2, 3], banks[4], src[1][:])
+        for r, bank in ((3, banks[5]), (0, banks[6])):
+            for b in range(4):
+                nc.tensor.transpose(bank[:, P * b : P * (b + 1)], turned[b][:, r, :], ident[:])
         nc.scalar.copy(src[0][:], banks[5][:])
         nc.vector.tensor_copy(a_win[3][:].indirect(list_a[:]), src[0][:])
         for r in (1, 2, 3):
@@ -173,45 +186,64 @@ def tile_moe_pool_relu_kernel(
             nc.scalar.copy(c_all[:, T * r : T * (r + 1)], c_win[r][:, 0:T])
         nc.scalar.copy(src[1][:], banks[6][:])
         nc.vector.tensor_copy(a_all[:].indirect(list_a[:]), src[1][:])
-
-        a4 = a_all[:].rearrange("p (r c i) -> p c r i", r=4, i=4)
-        c4 = c_all[:].rearrange("p (r c i) -> p c r i", r=4, i=4)
-        out_v = out.rearrange("(n p) t -> p n t", p=P)
-        hs = []
-        t0 = 0
-        for j, w in enumerate(CHUNKS):
-            h = tile([P, 4 * w], BF16, "h%d" % j)
-            cs = slice(t0 // 4, (t0 + w) // 4)
-            nc.vector.tensor_tensor(
-                h[:].rearrange("p (c i r) -> p c r i", i=4, r=4), a4[:, cs, :, :], c4[:, cs, :, :], MULT
+        nc.tensor.transpose(banks[7][:, 0:P], c_all[:, 3 * T : 3 * T + P], ident[:])
+        for j in range(WARM):
+            nc.tensor.matmul_mx(
+                out=banks[7][:],
+                lhsT=w2[:, 0:P].bitcast(FP8X4),
+                lhsT_scale=w2s[:, 0:P],
+                rhs=w2[:].bitcast(FP8X4),
+                rhs_scale=w2s,
+                start=True,
+                stop=True,
             )
-            hs.append((h, t0, w))
-            t0 = t0 + w
-        bank_at = 0
-        for j, (h, t0, w) in enumerate(hs):
-            hq = tile([P, w], U32, "hq%d" % j)
-            hq_s = tile([P, w], U8, "hq_s%d" % j)
-            nc.vector.quantize_mx(out=hq[:].bitcast(FP8X4), scales=hq_s[:], in_=h[:])
+
+        a4 = a_all[:].rearrange("p (r c i) -> p c r i", r=4, i=RUN)
+        c4 = c_all[:].rearrange("p (r c i) -> p c r i", r=4, i=RUN)
+        out_v = out.rearrange("(n p) t -> p n t", p=P)
+        starts = [sum(CHUNKS[:j]) for j in range(len(CHUNKS))]
+        h = [tile([P, 4 * w], BF16, "h%d" % j) for j, w in enumerate(CHUNKS)]
+        hq = [tile([P, w], U32, "hq%d" % j) for j, w in enumerate(CHUNKS)]
+        hq_s = [tile([P, w], U8, "hq_s%d" % j) for j, w in enumerate(CHUNKS)]
+
+        def gate(j):
+            cs = slice(starts[j] // RUN, (starts[j] + CHUNKS[j]) // RUN)
+            nc.vector.tensor_tensor(
+                h[j][:].rearrange("p (c i r) -> p c r i", i=RUN, r=4), a4[:, cs, :, :], c4[:, cs, :, :], MULT
+            )
+
+        def quantise(j):
+            nc.vector.quantize_mx(out=hq[j][:].bitcast(FP8X4), scales=hq_s[j][:], in_=h[j][:])
+
+        def project(j, first_bank, per_bank, shared):
+            w, t0 = CHUNKS[j], starts[j]
             res = tile([P, 4, w], F32, "res%d" % j)
-            last = j == len(hs) - 1
-            per_bank = 2 if (w == 256 or last) else 4
-            for n0 in range(0, 4, per_bank):
-                acc = banks[bank_at]
-                bank_at = bank_at + 1
+            for g, n0 in enumerate(range(0, 4, per_bank)):
+                acc = banks[first_bank + g]
                 for n in range(n0, n0 + per_bank):
                     nc.tensor.matmul_mx(
                         out=acc[:, w * (n - n0) : w * (n - n0 + 1)],
                         lhsT=w2[:, P * n : P * (n + 1)].bitcast(FP8X4),
                         lhsT_scale=w2s[:, P * n : P * (n + 1)],
-                        rhs=hq[:].bitcast(FP8X4),
-                        rhs_scale=hq_s[:],
+                        rhs=hq[j][:].bitcast(FP8X4),
+                        rhs_scale=hq_s[j][:],
                         start=True,
                         stop=True,
                     )
                 got = acc[:, 0 : w * per_bank].rearrange("p (n t) -> p n t", t=w)
                 dst = res[:, n0 : n0 + per_bank, :]
-                if last and n0 > 0:
+                if shared and g % 2 == 1:
                     nc.vector.tensor_copy(dst, got)
                 else:
                     nc.scalar.copy(dst, got)
                 nc.sync.dma_start(out_v[:, n0 : n0 + per_bank, t0 : t0 + w], dst)
+
+        gate(0)
+        gate(1)
+        quantise(0)
+        quantise(1)
+        gate(2)
+        quantise(2)
+        project(0, 0, 2, False)
+        project(1, 2, 4, False)
+        project(2, 3, 1, True)

@@ -46,12 +46,12 @@ def tile_moe_pool_relu_kernel(
         xw_at = (T, 0)
         xs = tile([P, WIDE], U8, "xs")
         wa = [tile([P, PASSES, H], I32, "wa%d" % e) for e in range(E1)]
-        wsc = tile([P, (2 + E2 * PASSES) * H], U8, "wsc")
+        wsc = tile([P, (1 + E2 * PASSES) * H], U8, "wsc")
         was = wsc[:, 0:H]
-        w2s = wsc[:, H : 2 * H]
-        wbs = wsc[:, 2 * H :].rearrange("p (g i) -> p g i", i=H)
+        w2s = was
+        wbs = wsc[:, H:].rearrange("p (g i) -> p g i", i=H)
         wb = tile([P, E2 * PASSES, 2 * H], U8, "wb")
-        w2 = tile([P, N], I32, "w2")
+        w2 = wa[0][:, 0, :]
         xb_s1 = tile([P, T], U8, "xb_s1")
         ident = tile([P, P], F32, "ident")
 
@@ -88,11 +88,6 @@ def tile_moe_pool_relu_kernel(
             nc.sync.dma_start(
                 wbs[32 * q : 32 * q + 4, :, :].bitcast(I32), wbs_rows[4 * q : 4 * q + 4, :, :].bitcast(I32)
             )
-        nc.sync.dma_start(w2[:], w2_words[0].rearrange("p n d -> p (n d)").bitcast(I32))
-        for q in range(4):
-            nc.sync.dma_start(
-                w2s[32 * q : 32 * q + 4, :].bitcast(I32), w2_scales[0, 4 * q : 4 * q + 4, :].bitcast(I32)
-            )
 
         def x_window(s):
             return xw[:, xw_at[s] : xw_at[s] + WIDE].bitcast(U32)
@@ -115,7 +110,7 @@ def tile_moe_pool_relu_kernel(
         def by_plane(bank):
             return bank[:].rearrange("p (q r) -> p r q", r=4)
 
-        src = [tile([P, T], F32, "src%d" % i) for i in range(2)]
+        src = [tile([P, T], F32, "src%d" % i) for i in range(3)]
         a_all = tile([P, 4 * T], F32, "a_all")
         c_all = tile([P, 4 * T], F32, "c_all")
         a_win = {r: tile([P, WIDE], F32, "a_win%d" % r) for r in (1, 2, 3)}
@@ -154,18 +149,23 @@ def tile_moe_pool_relu_kernel(
         expert_a(2)
         expert_a(3)
         early_planes([2, 3], banks[4], src[1][:])
-        for r, bank in ((3, banks[5]), (0, banks[6])):
-            for b in range(4):
-                nc.tensor.transpose(bank[:, P * b : P * (b + 1)], turned[b][:, r, :], ident[:])
-        nc.scalar.copy(src[0][:], banks[5][:])
-        nc.vector.tensor_copy(a_win[3][:].indirect(list_a[:]), src[0][:])
+        for b in range(4):
+            nc.tensor.transpose(banks[5][:, P * b : P * (b + 1)], turned[b][:, 3, :], ident[:])
+        nc.scalar.copy(src[2][:], banks[5][:])
+        nc.vector.tensor_copy(a_win[3][:].indirect(list_a[:]), src[2][:])
         for r in (1, 2, 3):
             nc.sync.dma_start(a_all[:, T * r : T * (r + 1)], a_win[r][:, 0:T])
 
-        b_bank = [banks[7], banks[3], banks[4], banks[5]]
+        nc.sync.dma_start(w2, w2_words[0].rearrange("p n d -> p (n d)").bitcast(I32))
+        for q in range(4):
+            nc.sync.dma_start(
+                w2s[32 * q : 32 * q + 4, :].bitcast(I32), w2_scales[0, 4 * q : 4 * q + 4, :].bitcast(I32)
+            )
+
+        b_bank = [banks[7], banks[3], banks[2], banks[4]]
         for f in range(E2):
             cols = slice(P * f, P * (f + 1))
-            acc = banks[(4 + f) % 3]
+            acc = banks[f % 2]
             for s in range(PASSES):
                 nc.tensor.matmul_mx(
                     out=acc[:],
@@ -177,22 +177,33 @@ def tile_moe_pool_relu_kernel(
                     stop=(s == PASSES - 1),
                 )
             nc.scalar.copy(turned[4 + f][:], by_plane(acc))
-            for r in range(4):
-                nc.tensor.transpose(b_bank[r][:, cols], turned[4 + f][:, r, :], ident[:])
-        for r in range(4):
-            stage = src[(r + 1) % 2]
-            nc.scalar.copy(stage[:], b_bank[r][:])
-            nc.vector.tensor_copy(c_win[r][:].indirect(list_b[:]), stage[:])
+            nc.tensor.transpose(b_bank[0][:, cols], turned[4 + f][:, 0, :], ident[:])
+        for r in (1, 2, 3):
+            for f in range(E2):
+                nc.tensor.transpose(b_bank[r][:, P * f : P * (f + 1)], turned[4 + f][:, r, :], ident[:])
+        for b in range(4):
+            nc.tensor.transpose(banks[6][:, P * b : P * (b + 1)], turned[b][:, 0, :], ident[:])
+
+        def join_c(r):
             nc.scalar.copy(c_all[:, T * r : T * (r + 1)], c_win[r][:, 0:T])
-        nc.scalar.copy(src[1][:], banks[6][:])
-        nc.vector.tensor_copy(a_all[:].indirect(list_a[:]), src[1][:])
+
+        for r in range(4):
+            stage = src[r % 3]
+            nc.scalar.copy(stage[:], b_bank[r][:])
+            if r >= 2:
+                join_c(r - 2)
+            nc.vector.tensor_copy(c_win[r][:].indirect(list_b[:]), stage[:])
+        nc.scalar.copy(src[2][:], banks[6][:])
+        join_c(2)
+        nc.vector.tensor_copy(a_all[:].indirect(list_a[:]), src[2][:])
+        join_c(3)
         nc.tensor.transpose(banks[7][:, 0:P], c_all[:, 3 * T : 3 * T + P], ident[:])
         for j in range(WARM):
             nc.tensor.matmul_mx(
                 out=banks[7][:],
                 lhsT=w2[:, 0:P].bitcast(FP8X4),
                 lhsT_scale=w2s[:, 0:P],
-                rhs=w2[:].bitcast(FP8X4),
+                rhs=w2.bitcast(FP8X4),
                 rhs_scale=w2s,
                 start=True,
                 stop=True,

@@ -4,7 +4,7 @@ import concourse.mybir as mybir
 from concourse.masks import make_identity
 
 K, T, H, N = 1024, 512, 512, 512
-E1, C1, E2, C2 = 2, 256, 4, 128
+E1, C1, E2 = 2, 256, 4
 FLOPS = 2 * T * (2 * K * H + H * N)
 
 F32 = mybir.dt.float32
@@ -20,8 +20,10 @@ MULT = mybir.AluOpType.mult
 
 P = 128
 PASSES = 2
+PLANES = 4
+QUADRANTS = 4
+BLOCKS = T // P
 WIDE = 704
-WARM = 5
 RUN = 2
 CHUNKS = (128, 128, 256)
 
@@ -69,22 +71,22 @@ def tile_moe_pool_relu_kernel(
 
         nc.sync.dma_start(list_a[:], offs)
         load_x(0)
-        for q in range(4):
+        for q in range(QUADRANTS):
             nc.sync.dma_start(
-                xs[32 * q : 32 * q + 8, 0:T].bitcast(I32), x_scales[:, 4 * q : 4 * q + 4, :].bitcast(I32)
+                xs[32 * q : 32 * q + 4 * PASSES, 0:T].bitcast(I32), x_scales[:, 4 * q : 4 * q + 4, :].bitcast(I32)
             )
         load_x(1)
         load_wa(0)
         was_rows = wa_scales.rearrange("e s b i -> (e s) b i")
-        for q in range(4):
+        for q in range(QUADRANTS):
             nc.sync.dma_start(
-                was[32 * q : 32 * q + 16, :].bitcast(I32), was_rows[:, 4 * q : 4 * q + 4, :].bitcast(I32)
+                was[32 * q : 32 * q + 4 * E1 * PASSES, :].bitcast(I32), was_rows[:, 4 * q : 4 * q + 4, :].bitcast(I32)
             )
         nc.sync.dma_start(list_b[:], offs2)
         load_wa(1)
         nc.sync.dma_start(wb[:].bitcast(I32), wb_words.rearrange("f s p b -> p (f s) b").bitcast(I32))
         wbs_rows = wb_scales.rearrange("f s b i -> b (f s) i")
-        for q in range(4):
+        for q in range(QUADRANTS):
             nc.sync.dma_start(
                 wbs[32 * q : 32 * q + 4, :, :].bitcast(I32), wbs_rows[4 * q : 4 * q + 4, :, :].bitcast(I32)
             )
@@ -97,7 +99,8 @@ def tile_moe_pool_relu_kernel(
         nc.vector.tensor_copy(xa[0][:], x_window(0).indirect(list_a[:]))
         nc.vector.tensor_copy(xa_s[:], xs[:].indirect(list_a[:]))
         for e in range(E1):
-            nc.vector.tensor_copy(xa[1][:, C1 * e : C1 * (e + 1)], x_window(1).indirect(list_a[:, 16 * e : 16 * (e + 1)]))
+            entries = list_a[:, C1 // 16 * e : C1 // 16 * (e + 1)]
+            nc.vector.tensor_copy(xa[1][:, C1 * e : C1 * (e + 1)], x_window(1).indirect(entries))
         xb = [tile([P, T], U32, "xb%d" % s) for s in range(PASSES)]
         xb_s = tile([P, T], U8, "xb_s")
         nc.vector.tensor_copy(xb_s[:], xs[:].indirect(list_b[:]))
@@ -105,27 +108,31 @@ def tile_moe_pool_relu_kernel(
         for s in range(PASSES):
             nc.vector.tensor_copy(xb[s][:], x_window(s).indirect(list_b[:]))
 
-        turned = [tile([P, 4, P], F32, "turned%d" % b) for b in range(8)]
+        turned = [tile([P, PLANES, P], F32, "turned%d" % b) for b in range(2 * BLOCKS)]
 
         def by_plane(bank):
-            return bank[:].rearrange("p (q r) -> p r q", r=4)
+            return bank[:].rearrange("slot (p r) -> slot r p", r=PLANES)
 
         src = [tile([P, T], F32, "src%d" % i) for i in range(3)]
-        a_all = tile([P, 4 * T], F32, "a_all")
-        c_all = tile([P, 4 * T], F32, "c_all")
+        a_all = tile([P, PLANES * T], F32, "a_all")
+        c_all = tile([P, PLANES * T], F32, "c_all")
         a_win = {r: tile([P, WIDE], F32, "a_win%d" % r) for r in (1, 2, 3)}
-        c_win = [tile([P, WIDE], F32, "c_win%d" % r) for r in range(4)]
+        c_win = [tile([P, WIDE], F32, "c_win%d" % r) for r in range(PLANES)]
+
+        sums = banks[0:2]
+        a_plane3, a_plane0 = banks[5], banks[6]
+        c_planes = [banks[7], banks[3], banks[2], banks[4]]
 
         def expert_a(b):
             e, cols = b // 2, slice(P * b, P * (b + 1))
-            acc = banks[b % 2]
+            acc = sums[b % 2]
             for s in range(PASSES):
                 nc.tensor.matmul_mx(
                     out=acc[:],
                     lhsT=xa[s][:, cols].bitcast(FP8X4),
                     lhsT_scale=xa_s[4 * s : P, cols],
                     rhs=wa[e][:, s, :].bitcast(FP8X4),
-                    rhs_scale=was[4 * (2 * e + s) : P, :],
+                    rhs_scale=was[4 * (PASSES * e + s) : P, :],
                     start=(s == 0),
                     stop=(s == PASSES - 1),
                 )
@@ -138,9 +145,9 @@ def tile_moe_pool_relu_kernel(
                     c0 = w * (r - 1) + P * j
                     nc.tensor.transpose(bank[:, c0 : c0 + P], turned[b][:, r, :], ident[:])
             nc.scalar.copy(stage, bank[:, 0 : 2 * w])
-            part = list_a[:, 8 * blocks[0] : 8 * (blocks[-1] + 1)]
+            entries = list_a[:, P // 16 * blocks[0] : P // 16 * (blocks[-1] + 1)]
             for r in (1, 2):
-                nc.vector.tensor_copy(a_win[r][:].indirect(part), stage[:, w * (r - 1) : w * r])
+                nc.vector.tensor_copy(a_win[r][:].indirect(entries), stage[:, w * (r - 1) : w * r])
 
         expert_a(0)
         expert_a(1)
@@ -149,87 +156,78 @@ def tile_moe_pool_relu_kernel(
         expert_a(2)
         expert_a(3)
         early_planes([2, 3], banks[4], src[1][:])
-        for b in range(4):
-            nc.tensor.transpose(banks[5][:, P * b : P * (b + 1)], turned[b][:, 3, :], ident[:])
-        nc.scalar.copy(src[2][:], banks[5][:])
+        for b in range(BLOCKS):
+            nc.tensor.transpose(a_plane3[:, P * b : P * (b + 1)], turned[b][:, 3, :], ident[:])
+        nc.scalar.copy(src[2][:], a_plane3[:])
         nc.vector.tensor_copy(a_win[3][:].indirect(list_a[:]), src[2][:])
         for r in (1, 2, 3):
             nc.sync.dma_start(a_all[:, T * r : T * (r + 1)], a_win[r][:, 0:T])
 
         nc.sync.dma_start(w2, w2_words[0].rearrange("p n d -> p (n d)").bitcast(I32))
-        for q in range(4):
+        for q in range(QUADRANTS):
             nc.sync.dma_start(
                 w2s[32 * q : 32 * q + 4, :].bitcast(I32), w2_scales[0, 4 * q : 4 * q + 4, :].bitcast(I32)
             )
 
-        b_bank = [banks[7], banks[3], banks[2], banks[4]]
         for f in range(E2):
             cols = slice(P * f, P * (f + 1))
-            acc = banks[f % 2]
+            acc = sums[f % 2]
             for s in range(PASSES):
                 nc.tensor.matmul_mx(
                     out=acc[:],
                     lhsT=xb[s][:, cols].bitcast(FP8X4),
                     lhsT_scale=(xb_s, xb_s1)[s][:, cols],
-                    rhs=wb[:, 2 * f + s, :].bitcast(FP4X4),
-                    rhs_scale=wbs[:, 2 * f + s, :],
+                    rhs=wb[:, PASSES * f + s, :].bitcast(FP4X4),
+                    rhs_scale=wbs[:, PASSES * f + s, :],
                     start=(s == 0),
                     stop=(s == PASSES - 1),
                 )
-            nc.scalar.copy(turned[4 + f][:], by_plane(acc))
-            nc.tensor.transpose(b_bank[0][:, cols], turned[4 + f][:, 0, :], ident[:])
+            nc.scalar.copy(turned[BLOCKS + f][:], by_plane(acc))
+            nc.tensor.transpose(c_planes[0][:, cols], turned[BLOCKS + f][:, 0, :], ident[:])
         for r in (1, 2, 3):
             for f in range(E2):
-                nc.tensor.transpose(b_bank[r][:, P * f : P * (f + 1)], turned[4 + f][:, r, :], ident[:])
-        for b in range(4):
-            nc.tensor.transpose(banks[6][:, P * b : P * (b + 1)], turned[b][:, 0, :], ident[:])
+                nc.tensor.transpose(c_planes[r][:, P * f : P * (f + 1)], turned[BLOCKS + f][:, r, :], ident[:])
+        for b in range(BLOCKS):
+            nc.tensor.transpose(a_plane0[:, P * b : P * (b + 1)], turned[b][:, 0, :], ident[:])
 
         def join_c(r):
             nc.scalar.copy(c_all[:, T * r : T * (r + 1)], c_win[r][:, 0:T])
 
-        for r in range(4):
-            stage = src[r % 3]
-            nc.scalar.copy(stage[:], b_bank[r][:])
+        for r in range(PLANES):
+            stage = src[r % len(src)]
+            nc.scalar.copy(stage[:], c_planes[r][:])
             if r >= 2:
                 join_c(r - 2)
             nc.vector.tensor_copy(c_win[r][:].indirect(list_b[:]), stage[:])
-        nc.scalar.copy(src[2][:], banks[6][:])
+        nc.scalar.copy(src[2][:], a_plane0[:])
         join_c(2)
         nc.vector.tensor_copy(a_all[:].indirect(list_a[:]), src[2][:])
         join_c(3)
-        nc.tensor.transpose(banks[7][:, 0:P], c_all[:, 3 * T : 3 * T + P], ident[:])
-        for j in range(WARM):
-            nc.tensor.matmul_mx(
-                out=banks[7][:],
-                lhsT=w2[:, 0:P].bitcast(FP8X4),
-                lhsT_scale=w2s[:, 0:P],
-                rhs=w2.bitcast(FP8X4),
-                rhs_scale=w2s,
-                start=True,
-                stop=True,
-            )
 
-        a4 = a_all[:].rearrange("p (r c i) -> p c r i", r=4, i=RUN)
-        c4 = c_all[:].rearrange("p (r c i) -> p c r i", r=4, i=RUN)
-        out_v = out.rearrange("(n p) t -> p n t", p=P)
+        a_runs = a_all[:].rearrange("p (r c u) -> p c r u", r=PLANES, u=RUN)
+        c_runs = c_all[:].rearrange("p (r c u) -> p c r u", r=PLANES, u=RUN)
+        out_rows = out.rearrange("(n p) t -> p n t", p=P)
         starts = [sum(CHUNKS[:j]) for j in range(len(CHUNKS))]
-        h = [tile([P, 4 * w], BF16, "h%d" % j) for j, w in enumerate(CHUNKS)]
+        h = [tile([P, PLANES * w], BF16, "h%d" % j) for j, w in enumerate(CHUNKS)]
         hq = [tile([P, w], U32, "hq%d" % j) for j, w in enumerate(CHUNKS)]
         hq_s = [tile([P, w], U8, "hq_s%d" % j) for j, w in enumerate(CHUNKS)]
 
         def gate(j):
-            cs = slice(starts[j] // RUN, (starts[j] + CHUNKS[j]) // RUN)
+            runs = slice(starts[j] // RUN, (starts[j] + CHUNKS[j]) // RUN)
             nc.vector.tensor_tensor(
-                h[j][:].rearrange("p (c i r) -> p c r i", i=RUN, r=4), a4[:, cs, :, :], c4[:, cs, :, :], MULT
+                h[j][:].rearrange("p (c u r) -> p c r u", u=RUN, r=PLANES),
+                a_runs[:, runs, :, :],
+                c_runs[:, runs, :, :],
+                MULT,
             )
 
         def quantise(j):
             nc.vector.quantize_mx(out=hq[j][:].bitcast(FP8X4), scales=hq_s[j][:], in_=h[j][:])
 
-        def project(j, first_bank, per_bank, shared):
+        def project(j, first_bank, per_bank, engines):
             w, t0 = CHUNKS[j], starts[j]
-            res = tile([P, 4, w], F32, "res%d" % j)
-            for g, n0 in enumerate(range(0, 4, per_bank)):
+            res = tile([P, N // P, w], F32, "res%d" % j)
+            for g, n0 in enumerate(range(0, N // P, per_bank)):
                 acc = banks[first_bank + g]
                 for n in range(n0, n0 + per_bank):
                     nc.tensor.matmul_mx(
@@ -241,13 +239,9 @@ def tile_moe_pool_relu_kernel(
                         start=True,
                         stop=True,
                     )
-                got = acc[:, 0 : w * per_bank].rearrange("p (n t) -> p n t", t=w)
                 dst = res[:, n0 : n0 + per_bank, :]
-                if shared and g % 2 == 1:
-                    nc.vector.tensor_copy(dst, got)
-                else:
-                    nc.scalar.copy(dst, got)
-                nc.sync.dma_start(out_v[:, n0 : n0 + per_bank, t0 : t0 + w], dst)
+                engines[g % len(engines)](dst, acc[:, 0 : w * per_bank].rearrange("p (n t) -> p n t", t=w))
+                nc.sync.dma_start(out_rows[:, n0 : n0 + per_bank, t0 : t0 + w], dst)
 
         gate(0)
         gate(1)
@@ -255,6 +249,6 @@ def tile_moe_pool_relu_kernel(
         quantise(1)
         gate(2)
         quantise(2)
-        project(0, 0, 2, False)
-        project(1, 2, 4, False)
-        project(2, 3, 1, True)
+        project(0, 0, 2, [nc.scalar.copy])
+        project(1, 2, 4, [nc.scalar.copy])
+        project(2, 3, 1, [nc.scalar.copy, nc.vector.tensor_copy])

from contextlib import ExitStack

import concourse.mybir as mybir
from concourse.masks import make_identity

K, T, H, N = 1024, 512, 512, 512
E1, C1, E2 = 2, 256, 4
FLOPS = 2 * T * (2 * K * H + H * N)

F32 = mybir.dt.float32
BF16 = mybir.dt.bfloat16
I32 = mybir.dt.int32
U32 = mybir.dt.uint32
U16 = mybir.dt.uint16
U8 = mybir.dt.uint8
FP8X4 = mybir.dt.float8_e4m3fn_x4
FP4X4 = mybir.dt.float4_e2m1fn_x4
RELU = mybir.ActivationFunctionType.Relu
MULT = mybir.AluOpType.mult

P = 128
PASSES = 2
PLANES = 4
QUADRANTS = 4
BLOCKS = T // P
WIDE = 704
RUN = 2
CHUNKS = (128, 128, 256)


def tile_moe_pool_relu_kernel(
    tc, x_words, x_scales, wa_words, wa_scales, wb_words, wb_scales, w2_words, w2_scales, offs, offs2, out
):
    nc = tc.nc
    with ExitStack() as ctx:
        lists = ctx.enter_context(tc.tile_pool(name="lists", bufs=1))
        sb = ctx.enter_context(tc.tile_pool(name="sb", bufs=1))
        ps = ctx.enter_context(tc.psum_pool(name="ps", bufs=1))

        def tile(shape, dtype, name):
            return sb.tile(shape, dtype, name=name, align_bytes=64)

        list_a = lists.tile([P, T // 16], U16, name="list_a")
        list_b = lists.tile([P, T // 16], U16, name="list_b")
        banks = [ps.tile([P, 512], F32, name="bank%d" % b) for b in range(8)]

        xw = tile([P, T + WIDE], I32, "xw")
        xw_at = (T, 0)
        xs = tile([P, WIDE], U8, "xs")
        wa = [tile([P, PASSES, H], I32, "wa%d" % e) for e in range(E1)]
        wsc = tile([P, (1 + E2 * PASSES) * H], U8, "wsc")
        was = wsc[:, 0:H]
        w2s = was
        wbs = wsc[:, H:].rearrange("p (g i) -> p g i", i=H)
        wb = tile([P, E2 * PASSES, 2 * H], U8, "wb")
        w2 = wa[0][:, 0, :]
        xb_s1 = tile([P, T], U8, "xb_s1")
        ident = tile([P, P], F32, "ident")

        nc.vector.memset(xs[:].bitcast(I32), 0)
        nc.vector.memset(xw[:, 2 * T : T + WIDE], 0)
        nc.vector.memset(wsc[:].bitcast(I32), 0)
        nc.vector.memset(xb_s1[:].bitcast(I32), 0)
        make_identity(nc, ident[:])

        def load_x(s):
            nc.sync.dma_start(xw[:, xw_at[s] : xw_at[s] + T], x_words[s].rearrange("p t d -> p (t d)").bitcast(I32))

        def load_wa(e):
            nc.sync.dma_start(wa[e][:], wa_words[e].rearrange("s p i d -> p s (i d)").bitcast(I32))

        nc.sync.dma_start(list_a[:], offs)
        load_x(0)
        for q in range(QUADRANTS):
            nc.sync.dma_start(
                xs[32 * q : 32 * q + 4 * PASSES, 0:T].bitcast(I32), x_scales[:, 4 * q : 4 * q + 4, :].bitcast(I32)
            )
        load_x(1)
        load_wa(0)
        was_rows = wa_scales.rearrange("e s b i -> (e s) b i")
        for q in range(QUADRANTS):
            nc.sync.dma_start(
                was[32 * q : 32 * q + 4 * E1 * PASSES, :].bitcast(I32), was_rows[:, 4 * q : 4 * q + 4, :].bitcast(I32)
            )
        nc.sync.dma_start(list_b[:], offs2)
        load_wa(1)
        nc.sync.dma_start(wb[:].bitcast(I32), wb_words.rearrange("f s p b -> p (f s) b").bitcast(I32))
        wbs_rows = wb_scales.rearrange("f s b i -> b (f s) i")
        for q in range(QUADRANTS):
            nc.sync.dma_start(
                wbs[32 * q : 32 * q + 4, :, :].bitcast(I32), wbs_rows[4 * q : 4 * q + 4, :, :].bitcast(I32)
            )

        def x_window(s):
            return xw[:, xw_at[s] : xw_at[s] + WIDE].bitcast(U32)

        xa = [tile([P, T], U32, "xa%d" % s) for s in range(PASSES)]
        xa_s = tile([P, T], U8, "xa_s")
        nc.vector.tensor_copy(xa[0][:], x_window(0).indirect(list_a[:]))
        nc.vector.tensor_copy(xa_s[:], xs[:].indirect(list_a[:]))
        for e in range(E1):
            entries = list_a[:, C1 // 16 * e : C1 // 16 * (e + 1)]
            nc.vector.tensor_copy(xa[1][:, C1 * e : C1 * (e + 1)], x_window(1).indirect(entries))
        xb = [tile([P, T], U32, "xb%d" % s) for s in range(PASSES)]
        xb_s = tile([P, T], U8, "xb_s")
        nc.vector.tensor_copy(xb_s[:], xs[:].indirect(list_b[:]))
        nc.sync.dma_start(xb_s1[0 : P - 4, :].bitcast(I32), xb_s[4:P, :].bitcast(I32))
        for s in range(PASSES):
            nc.vector.tensor_copy(xb[s][:], x_window(s).indirect(list_b[:]))

        turned = [tile([P, PLANES, P], F32, "turned%d" % b) for b in range(2 * BLOCKS)]

        def by_plane(bank):
            return bank[:].rearrange("slot (p r) -> slot r p", r=PLANES)

        src = [tile([P, T], F32, "src%d" % i) for i in range(3)]
        a_all = tile([P, PLANES * T], F32, "a_all")
        c_all = tile([P, PLANES * T], F32, "c_all")
        a_win = {r: tile([P, WIDE], F32, "a_win%d" % r) for r in (1, 2, 3)}
        c_win = [tile([P, WIDE], F32, "c_win%d" % r) for r in range(PLANES)]

        sums = banks[0:2]
        a_plane3, a_plane0 = banks[5], banks[6]
        c_planes = [banks[7], banks[3], banks[2], banks[4]]

        def expert_a(b):
            e, cols = b // 2, slice(P * b, P * (b + 1))
            acc = sums[b % 2]
            for s in range(PASSES):
                nc.tensor.matmul_mx(
                    out=acc[:],
                    lhsT=xa[s][:, cols].bitcast(FP8X4),
                    lhsT_scale=xa_s[4 * s : P, cols],
                    rhs=wa[e][:, s, :].bitcast(FP8X4),
                    rhs_scale=was[4 * (PASSES * e + s) : P, :],
                    start=(s == 0),
                    stop=(s == PASSES - 1),
                )
            nc.scalar.activation(turned[b][:], by_plane(acc), RELU)

        def early_planes(blocks, bank, stage):
            w = P * len(blocks)
            for j, b in enumerate(blocks):
                for r in (1, 2):
                    c0 = w * (r - 1) + P * j
                    nc.tensor.transpose(bank[:, c0 : c0 + P], turned[b][:, r, :], ident[:])
            nc.scalar.copy(stage, bank[:, 0 : 2 * w])
            entries = list_a[:, P // 16 * blocks[0] : P // 16 * (blocks[-1] + 1)]
            for r in (1, 2):
                nc.vector.tensor_copy(a_win[r][:].indirect(entries), stage[:, w * (r - 1) : w * r])

        expert_a(0)
        expert_a(1)
        early_planes([0], banks[7], src[0][:, 0 : 2 * P])
        early_planes([1], banks[3], src[0][:, 2 * P : 4 * P])
        expert_a(2)
        expert_a(3)
        early_planes([2, 3], banks[4], src[1][:])
        for b in range(BLOCKS):
            nc.tensor.transpose(a_plane3[:, P * b : P * (b + 1)], turned[b][:, 3, :], ident[:])
        nc.scalar.copy(src[2][:], a_plane3[:])
        nc.vector.tensor_copy(a_win[3][:].indirect(list_a[:]), src[2][:])
        for r in (1, 2, 3):
            nc.sync.dma_start(a_all[:, T * r : T * (r + 1)], a_win[r][:, 0:T])

        nc.sync.dma_start(w2, w2_words[0].rearrange("p n d -> p (n d)").bitcast(I32))
        for q in range(QUADRANTS):
            nc.sync.dma_start(
                w2s[32 * q : 32 * q + 4, :].bitcast(I32), w2_scales[0, 4 * q : 4 * q + 4, :].bitcast(I32)
            )

        for f in range(E2):
            cols = slice(P * f, P * (f + 1))
            acc = sums[f % 2]
            for s in range(PASSES):
                nc.tensor.matmul_mx(
                    out=acc[:],
                    lhsT=xb[s][:, cols].bitcast(FP8X4),
                    lhsT_scale=(xb_s, xb_s1)[s][:, cols],
                    rhs=wb[:, PASSES * f + s, :].bitcast(FP4X4),
                    rhs_scale=wbs[:, PASSES * f + s, :],
                    start=(s == 0),
                    stop=(s == PASSES - 1),
                )
            nc.scalar.copy(turned[BLOCKS + f][:], by_plane(acc))
            nc.tensor.transpose(c_planes[0][:, cols], turned[BLOCKS + f][:, 0, :], ident[:])
        for r in (1, 2, 3):
            for f in range(E2):
                nc.tensor.transpose(c_planes[r][:, P * f : P * (f + 1)], turned[BLOCKS + f][:, r, :], ident[:])
        for b in range(BLOCKS):
            nc.tensor.transpose(a_plane0[:, P * b : P * (b + 1)], turned[b][:, 0, :], ident[:])

        def join_c(r):
            nc.scalar.copy(c_all[:, T * r : T * (r + 1)], c_win[r][:, 0:T])

        for r in range(PLANES):
            stage = src[r % len(src)]
            nc.scalar.copy(stage[:], c_planes[r][:])
            if r >= 2:
                join_c(r - 2)
            nc.vector.tensor_copy(c_win[r][:].indirect(list_b[:]), stage[:])
        nc.scalar.copy(src[2][:], a_plane0[:])
        join_c(2)
        nc.vector.tensor_copy(a_all[:].indirect(list_a[:]), src[2][:])
        join_c(3)

        a_runs = a_all[:].rearrange("p (r c u) -> p c r u", r=PLANES, u=RUN)
        c_runs = c_all[:].rearrange("p (r c u) -> p c r u", r=PLANES, u=RUN)
        out_rows = out.rearrange("(n p) t -> p n t", p=P)
        starts = [sum(CHUNKS[:j]) for j in range(len(CHUNKS))]
        h = [tile([P, PLANES * w], BF16, "h%d" % j) for j, w in enumerate(CHUNKS)]
        hq = [tile([P, w], U32, "hq%d" % j) for j, w in enumerate(CHUNKS)]
        hq_s = [tile([P, w], U8, "hq_s%d" % j) for j, w in enumerate(CHUNKS)]

        def gate(j):
            runs = slice(starts[j] // RUN, (starts[j] + CHUNKS[j]) // RUN)
            nc.vector.tensor_tensor(
                h[j][:].rearrange("p (c u r) -> p c r u", u=RUN, r=PLANES),
                a_runs[:, runs, :, :],
                c_runs[:, runs, :, :],
                MULT,
            )

        def quantise(j):
            nc.vector.quantize_mx(out=hq[j][:].bitcast(FP8X4), scales=hq_s[j][:], in_=h[j][:])

        def project(j, first_bank, per_bank, engines):
            w, t0 = CHUNKS[j], starts[j]
            res = tile([P, N // P, w], F32, "res%d" % j)
            for g, n0 in enumerate(range(0, N // P, per_bank)):
                acc = banks[first_bank + g]
                for n in range(n0, n0 + per_bank):
                    nc.tensor.matmul_mx(
                        out=acc[:, w * (n - n0) : w * (n - n0 + 1)],
                        lhsT=w2[:, P * n : P * (n + 1)].bitcast(FP8X4),
                        lhsT_scale=w2s[:, P * n : P * (n + 1)],
                        rhs=hq[j][:].bitcast(FP8X4),
                        rhs_scale=hq_s[j][:],
                        start=True,
                        stop=True,
                    )
                dst = res[:, n0 : n0 + per_bank, :]
                engines[g % len(engines)](dst, acc[:, 0 : w * per_bank].rearrange("p (n t) -> p n t", t=w))
                nc.sync.dma_start(out_rows[:, n0 : n0 + per_bank, t0 : t0 + w], dst)

        gate(0)
        gate(1)
        quantise(0)
        quantise(1)
        gate(2)
        quantise(2)
        project(0, 0, 2, [nc.scalar.copy])
        project(1, 2, 4, [nc.scalar.copy])
        project(2, 3, 1, [nc.scalar.copy, nc.vector.tensor_copy])
